import numpy as np, ml_dtypes
CORES = [2,3,42,43,82,83,122,123]
N = 8
KB, QP = 1, 128
def setup_inputs(rng):
    q = rng.standard_normal((N, 128, QP), dtype=np.float32) / 4; k = rng.standard_normal((N, 128, KB * 128), dtype=np.float32)
    a = 2 * np.pi * rng.random((N, QP)); s = 400 * rng.random((N, QP)) ** 1.5; q[:, 0, :] = s * np.cos(a); q[:, 1, :] = s * np.sin(a); q[:, 2, :] = 150 * rng.standard_normal((N, QP)); k[:, 2, :] = 1 + k[:, 2, :] / 50
    a = (2 * np.pi * rng.random() + np.pi / 2 * (rng.permutation(N).reshape(N, 1, 1) + 0.5) / N - 0.5 + (np.arange(KB).reshape(1, KB, 1) + rng.random((N, KB, 128))) / KB).reshape(N, KB * 128); k[:, 0, :] = np.cos(a); k[:, 1, :] = np.sin(a)
    return {"q": q.astype(ml_dtypes.bfloat16), "k": k.astype(ml_dtypes.bfloat16), "v": rng.standard_normal((N, 128, KB * 128), dtype=np.float32).astype(ml_dtypes.bfloat16)}
def setup_inputs_big(rng):
    d = setup_inputs(rng)
    for k in ("v",): d[k] = (d[k].astype(np.float32) * 1048576.0).astype(d[k].dtype)
    return d
def setup_inputs_small(rng):
    d = setup_inputs(rng)
    for k in ("v",): d[k] = (d[k].astype(np.float32) * (1 / 1048576.0)).astype(d[k].dtype)
    return d
def reference(q, k, v):
    Q, K, V = q.astype(np.float64), k.astype(np.float64), v.astype(np.float64)
    y = np.zeros((N, QP, 128))
    for r in range(N):
        js = list(range(r + 1))
        S = np.concatenate([K[j].T @ Q[r] for j in js], axis=0)
        kp = np.concatenate([j * KB * 128 + np.arange(KB * 128) for j in js]); S = np.where(kp[:, None] <= (r * QP + np.arange(QP))[None, :], S, -np.inf)
        P = np.exp(S - S.max(axis=0)); P = P / P.sum(axis=0)
        y[r] = P.T @ np.concatenate([V[j][:, 128 * b:128 * b + 128] for j in js for b in range(KB)], axis=0)
    return {"y": y.astype(ml_dtypes.bfloat16)}

@@ -1,0 +1,301 @@
+from concourse.bass import DstId, RemoteDMATransfer
+from concourse.mybir import AluOpType, AxisListType, ActivationFunctionType
+
+N = 8
+NPOOL = 96
+
+SCRATCH = {
+    "qs": ("sbuf", [128, 128], "bfloat16"),
+    "kv": ("sbuf", [128, N * 256], "bfloat16"),
+    "ident": ("sbuf", [128, 128], "bfloat16"),
+    "maskb": ("sbuf", [128, 128], "bfloat16"),
+    "p": ("sbuf", [128, N * 128], "bfloat16"),
+    "pt": ("sbuf", [128, N * 128], "bfloat16"),
+    "dg": ("sbuf", [128, N * 128], "bfloat16"),
+    "op": ("sbuf", [128, N * 128], "bfloat16"),
+    "st": ("sbuf", [128, 96], "float32"),
+    "ys": ("sbuf", [128, 128], "bfloat16"),
+    "kvd": ("dram", [128, 256], "bfloat16"),
+    "landd": ("dram", [N, 128, 256], "bfloat16"),
+    "ps_s0": ("psum", [128, 512], "float32"),
+    "ps_s1": ("psum", [128, 512], "float32"),
+    "ps_t0": ("psum", [128, 1024], "bfloat16"),
+    "ps_t1": ("psum", [128, 1024], "bfloat16"),
+    "ps_o0": ("psum", [128, 512], "float32"),
+    "ps_o1": ("psum", [128, 512], "float32"),
+}
+SEMAPHORES = (["sent"] + ["ld%d" % j for j in range(N)] + ["fw%d" % j for j in range(N)]
+              + ["x%d" % i for i in range(NPOOL)])
+
+
+def _bits(mask):
+    return [b for b in range(mask.bit_length()) if (mask >> b) & 1]
+
+
+def _part(mask, k, parts):
+    bs = _bits(mask)
+    w = len(bs) // parts
+    return sum(1 << b for b in bs[k * w:(k + 1) * w])
+
+
+def rank_program(g, core, T, topo):
+    r = T.rank_of(core)
+    if r is None:
+        return
+    cores = list(T.cores)
+    n = len(cores)
+    chip_of = [topo.chip(c) for c in cores]
+    chips = []
+    for ch in chip_of:
+        if ch not in chips:
+            chips.append(ch)
+    members = {ch: [i for i in range(n) if chip_of[i] == ch] for ch in chips}
+    my_chip = chip_of[r]
+    my_pos = chips.index(my_chip)
+    later = chips[my_pos + 1:]
+    earlier = chips[:my_pos]
+    sibs = [i for i in members[my_chip] if i != r]
+
+    def lander(j, ch):
+        m = members[ch]
+        pos = members[chip_of[j]].index(j) % len(m)
+        if m[pos] == n - 1 and len(m) > 1:
+            pos -= 1
+        return m[pos]
+
+    def dst_id(c):
+        a = topo.addr(c)
+        return DstId(rid=a[0], pnc=a[1])
+
+    eng = {"pe": g.tensor, "dve": g.vector, "act": g.scalar, "sp": g.sync, "g": g}
+    seen = {k: {} for k in eng}
+    cnt = [0]
+
+    def need(q, toks):
+        for t in toks:
+            if t is None:
+                continue
+            nm, v = t
+            if seen[q].get(nm, 0) < v:
+                eng[q].wait_ge(T.sem[nm], v)
+                seen[q][nm] = v
+
+    def emit(q, toks, fn, inc=1, tok=None):
+        need(q, toks)
+        ins = fn()
+        if tok is None:
+            tok = ("x%d" % cnt[0], 0)
+            cnt[0] += 1
+        ins.then_inc(T.sem[tok[0]], inc)
+        return (tok[0], tok[1] + inc)
+
+    def slot(j):
+        return T.kv[:, j * 256:(j + 1) * 256]
+
+    def kslot(j):
+        return T.kv[:, j * 256:j * 256 + 128]
+
+    def vslot(j):
+        return T.kv[:, j * 256 + 128:(j + 1) * 256]
+
+    tk_sk = tk_sv = None
+    if later:
+        tk_sk = emit("sp", [], lambda: g.sync.dma_start(T.kvd[:, 0:128], T.k[:, :]), 16)
+        tk_sv = emit("act", [], lambda: g.scalar.dma_start(T.kvd[:, 128:256], T.v[:, :]), 16)
+    tk_k = emit("sp", [], lambda: g.sync.dma_start(kslot(r), T.k[:, :]), 16)
+    tk_v = emit("act", [], lambda: g.scalar.dma_start(vslot(r), T.v[:, :]), 16)
+    tk_q = emit("sp", [], lambda: g.sync.dma_start(T.qs[:, :], T.q[:, :]), 16)
+
+    t_one = emit("dve", [], lambda: g.vector.memset(T.ident[:, :], 1.0))
+    t_zero = emit("dve", [], lambda: g.vector.memset(T.maskb[:, :], 0.0))
+    tk_id = emit("g", [t_one], lambda: g.affine_select(T.ident[:, :], T.ident[:, :], [[-1, 128]],
+                                                       AluOpType.is_equal, 0.0, 0, 1))
+    tk_mk = emit("g", [t_zero], lambda: g.affine_select(T.maskb[:, :], T.maskb[:, :], [[-1, 128]],
+                                                        AluOpType.is_ge, -30000.0, 0, 1))
+
+    sent = 0
+    ready = {r: [tk_k, tk_v]}
+    if later:
+        need("g", [tk_sk, tk_sv])
+        dcs = [cores[lander(r, ch)] for ch in later]
+        m = topo.mask(core, dcs[0])
+        for d in dcs:
+            m &= topo.mask(core, d)
+        g.remote_dma_fused([RemoteDMATransfer(dst_ids=[dst_id(d) for d in dcs], dma_engine_mask=m,
+                                              remote_sem=T.sem["ld%d" % r], srcs=[T.kvd[:, :]],
+                                              dsts=[T.landd[r] for d in dcs], alu_op=0)], local_sem=T.sem.sent)
+        sent += len(_bits(m))
+    for i in sibs:
+        if i > r:
+            need("g", [tk_k, tk_v])
+            a = topo.addr(cores[i])
+            m = topo.mask(core, cores[i])
+            g.remote_dma(out_ap=slot(r), in_ap=slot(r), remote_sem=T.sem["fw%d" % r], local_sem=T.sem.sent,
+                         pid=a[1], routing_id=a[0], dma_engine_mask=m)
+            sent += len(_bits(m))
+        else:
+            ready[i] = [("fw%d" % i, len(_bits(topo.mask(cores[i], core))))]
+    for ch in reversed(earlier):
+        mine = [j for j in members[ch] if lander(j, my_chip) == r]
+        lds = {j: ("ld%d" % j, len(_bits(topo.mask(cores[j], core)))) for j in mine}
+        for j in mine:
+            ready[j] = [emit("sp", [lds[j]], lambda j=j: g.sync.dma_start(slot(j), T.landd[j]), 16)]
+        if mine and sibs:
+            need("g", [lds[j] for j in mine])
+            m = topo.mask(core, cores[sibs[0]])
+            for i in sibs:
+                m &= topo.mask(core, cores[i])
+            trs = []
+            for x, j in enumerate(mine):
+                mm = _part(m, x, len(mine))
+                trs.append(RemoteDMATransfer(dst_ids=[dst_id(cores[i]) for i in sibs], dma_engine_mask=mm,
+                                             remote_sem=T.sem["fw%d" % j], srcs=[T.landd[j]],
+                                             dsts=[slot(j) for i in sibs], alu_op=0))
+                sent += len(_bits(mm))
+            g.remote_dma_fused(trs, local_sem=T.sem.sent)
+        for j in members[ch]:
+            if j not in mine:
+                lr = lander(j, my_chip)
+                parts = len([x for x in members[ch] if lander(x, my_chip) == lr])
+                ready[j] = [("fw%d" % j, len(_bits(topo.mask(cores[lr], core))) // parts)]
+    if sent:
+        need("g", [("sent", sent)])
+
+    steps = [[r] + [i for i in sibs if i < r]] + [list(reversed(members[ch])) for ch in reversed(earlier)]
+    ns = len(steps)
+    ps_s = [T.ps_s0, T.ps_s1]
+    ps_t = [T.ps_t0, T.ps_t1]
+    ps_o = [T.ps_o0, T.ps_o1]
+    col = [0]
+
+    def cols(k=1):
+        c = col[0]
+        col[0] += k
+        return c
+
+    def st(c, k=1):
+        return T.st[:, c:c + k]
+
+    base = []
+    b0 = 0
+    for s in steps:
+        base.append(b0)
+        b0 += len(s)
+
+    def blk(buf, i):
+        return buf[:, i * 128:(i + 1) * 128]
+
+    X = [{} for _ in steps]
+
+    def scores(t):
+        S = ps_s[t % 2]
+        tok = None
+        for b, j in enumerate(steps[t]):
+            out = S[:, b * 128:(b + 1) * 128]
+            if j == r:
+                tok = emit("pe", [tk_id, tk_mk],
+                           lambda: g.tensor.matmul(out, T.ident[:, :], T.maskb[:, :], start=True, stop=False), 1, tok)
+                tok = emit("pe", [tk_q] + ready[j],
+                           lambda: g.tensor.matmul(out, T.qs[:, :], kslot(j), start=False, stop=True), 1, tok)
+            else:
+                tok = emit("pe", [tk_q] + ready[j],
+                           lambda: g.tensor.matmul(out, T.qs[:, :], kslot(j), start=True, stop=True), 1, tok)
+        X[t]["S"] = tok
+
+    def maxexp(t):
+        S = ps_s[t % 2]
+        nb = len(steps[t])
+        x = X[t]
+        c_m = cols()
+        tm = emit("dve", [x["S"]], lambda: g.vector.tensor_reduce(st(c_m), S[:, 0:nb * 128], axis=AxisListType.X,
+                                                                  op=AluOpType.max, negate=True))
+        if t == 0:
+            x["cM"], x["M"] = c_m, tm
+            x["cl"] = cols(nb)
+            x["nl"] = nb
+            l0 = x["cl"]
+        else:
+            pv = X[t - 1]
+            c_M = cols()
+            x["cM"] = c_M
+            x["M"] = emit("dve", [tm, pv["M"]], lambda: g.vector.tensor_tensor(st(c_M), st(c_m), st(pv["cM"]),
+                                                                              op=AluOpType.min))
+            c_w = cols()
+            x["cw"] = c_w
+            x["w"] = emit("act", [x["M"], pv["M"]],
+                          lambda: g.scalar.activation(st(c_w), st(pv["cM"]), ActivationFunctionType.Exp,
+                                                      bias=st(c_M), scale=-1.0))
+            x["cl"] = cols(nb + 1)
+            x["nl"] = nb + 1
+            l0 = x["cl"] + 1
+        x["E"] = []
+        for b in range(nb):
+            x["E"].append(emit("act", [x["M"], x["S"]],
+                               lambda b=b: g.scalar.activation(blk(T.p, base[t] + b), S[:, b * 128:(b + 1) * 128],
+                                                               ActivationFunctionType.Exp, bias=st(x["cM"]),
+                                                               scale=1.0, accum_out=st(l0 + b))))
+
+    def rescale_prep(t):
+        x, pv = X[t], X[t - 1]
+        x["dg"] = emit("dve", [x["w"], tk_id],
+                       lambda: g.vector.tensor_scalar(blk(T.dg, t), T.ident[:, :], st(x["cw"]), None,
+                                                      op0=AluOpType.mult))
+        x["lw"] = emit("dve", [x["w"], pv["L"]],
+                       lambda: g.vector.tensor_scalar(st(x["cl"]), st(pv["cL"]), st(x["cw"]), None,
+                                                      op0=AluOpType.mult))
+
+    def transposes(t):
+        x = X[t]
+        x["C"] = []
+        tts = []
+        for b in range(len(steps[t])):
+            tts.append(emit("pe", [x["E"][b], tk_id],
+                            lambda b=b: g.tensor.transpose(ps_t[b % 2][:, 0:128], blk(T.p, base[t] + b),
+                                                           T.ident[:, :])))
+        for b in range(len(steps[t])):
+            x["C"].append(emit("dve", [tts[b]],
+                               lambda b=b: g.vector.tensor_copy(blk(T.pt, base[t] + b), ps_t[b % 2][:, 0:128])))
+        c_L = cols()
+        x["cL"] = c_L
+        x["L"] = emit("dve", x["E"] + [x.get("lw")],
+                      lambda: g.vector.tensor_reduce(st(c_L), st(x["cl"], x["nl"]), axis=AxisListType.X,
+                                                     op=AluOpType.add))
+
+    def outputs(t):
+        x = X[t]
+        O = ps_o[t % 2][:, 0:128]
+        nb = len(steps[t])
+        tok = None
+        if t > 0:
+            tok = emit("pe", [x["dg"], X[t - 1]["O"]],
+                       lambda: g.tensor.matmul(O, blk(T.dg, t), blk(T.op, t - 1), start=True, stop=False), 1, tok)
+        for b, j in enumerate(steps[t]):
+            tok = emit("pe", [x["C"][b]] + ready[j],
+                       lambda b=b, j=j: g.tensor.matmul(O, blk(T.pt, base[t] + b), vslot(j),
+                                                        start=(t == 0 and b == 0), stop=(b == nb - 1)), 1, tok)
+        if t + 1 < ns:
+            x["O"] = emit("dve", [tok], lambda: g.vector.tensor_copy(blk(T.op, t), O))
+        else:
+            c_r = cols()
+            tr = emit("dve", [x["L"]], lambda: g.vector.reciprocal(st(c_r), st(x["cL"])))
+            ty = emit("dve", [tr, tok], lambda: g.vector.tensor_scalar(T.ys[:, :], O, st(c_r), None,
+                                                                       op0=AluOpType.mult))
+            td = emit("sp", [ty], lambda: g.sync.dma_start(T.y[:, :], T.ys[:, :]), 16)
+            need("sp", [td])
+
+    scores(0)
+    maxexp(0)
+    transposes(0)
+    outputs(0)
+    if ns > 1:
+        scores(1)
+        maxexp(1)
+        rescale_prep(1)
+    for t in range(1, ns):
+        if t + 1 < ns:
+            scores(t + 1)
+            maxexp(t + 1)
+        transposes(t)
+        if t + 1 < ns:
+            rescale_prep(t + 1)
+        outputs(t)

@@ -24,7 +24,7 @@ SCRATCH = {
     "ps_o0": ("psum", [128, 512], "float32"),
     "ps_o1": ("psum", [128, 512], "float32"),
 }
-SEMAPHORES = (["sent"] + ["ld%d" % j for j in range(N)] + ["fw%d" % j for j in range(N)]
+SEMAPHORES = (["sent", "idr"] + ["ld%d" % j for j in range(N)] + ["fw%d" % j for j in range(N)]
               + ["x%d" % i for i in range(NPOOL)])
 
 
@@ -58,10 +58,31 @@ def rank_program(g, core, T, topo):
 
     def lander(j, ch):
         m = members[ch]
-        pos = members[chip_of[j]].index(j) % len(m)
-        if m[pos] == n - 1 and len(m) > 1:
-            pos -= 1
-        return m[pos]
+        return m[members[chip_of[j]].index(j) % len(m)]
+
+    def quiet(i):
+        ch = chip_of[i]
+        on = 0
+        for x in members[ch]:
+            if x != i:
+                mk = topo.mask(cores[i], cores[x])
+                on = mk if not on else on & mk
+        off = 0
+        for c2 in chips[chips.index(ch) + 1:]:
+            off |= topo.mask(cores[i], cores[lander(i, c2)])
+        rest = on & ~off
+        return rest if len(_bits(rest)) in (1, 2, 4, 8, 16) else on
+
+    def first(i):
+        ch = chip_of[i]
+        m = 0
+        for x in members[ch]:
+            if x != i:
+                mk = topo.mask(cores[i], cores[x])
+                m = mk if not m else m & mk
+        for c2 in chips[chips.index(ch) + 1:]:
+            m &= topo.mask(cores[i], cores[lander(i, c2)])
+        return m
 
     def dst_id(c):
         a = topo.addr(c)
@@ -106,14 +127,25 @@ def rank_program(g, core, T, topo):
     tk_v = emit("act", [], lambda: g.scalar.dma_start(vslot(r), T.v[:, :]), 16)
     tk_q = emit("sp", [], lambda: g.sync.dma_start(T.qs[:, :], T.q[:, :]), 16)
 
-    t_one = emit("dve", [], lambda: g.vector.memset(T.ident[:, :], 1.0))
-    t_zero = emit("dve", [], lambda: g.vector.memset(T.maskb[:, :], 0.0))
-    tk_id = emit("g", [t_one], lambda: g.affine_select(T.ident[:, :], T.ident[:, :], [[-1, 128]],
-                                                       AluOpType.is_equal, 0.0, 0, 1))
-    tk_mk = emit("g", [t_zero], lambda: g.affine_select(T.maskb[:, :], T.maskb[:, :], [[-1, 128]],
-                                                        AluOpType.is_ge, -30000.0, 0, 1))
-
+    grp = members[my_chip]
+    w_id = 128 // len(grp)
+    c0 = grp.index(r) * w_id
+    own_id = T.ident[:, c0:c0 + w_id]
     sent = 0
+    t_one = emit("dve", [], lambda: g.vector.memset(own_id, 1.0))
+    t_zero = emit("dve", [], lambda: g.vector.memset(T.maskb[:, :], 0.0))
+    t_own = emit("g", [t_one], lambda: g.affine_select(own_id, own_id, [[-1, w_id]],
+                                                       AluOpType.is_equal, 0.0, -c0, 1))
+    tk_id = [t_own]
+    if sibs:
+        need("g", [t_own])
+        for i in sibs:
+            a = topo.addr(cores[i])
+            g.remote_dma(out_ap=own_id, in_ap=own_id, remote_sem=T.sem.idr, local_sem=T.sem.sent,
+                         pid=a[1], routing_id=a[0], dma_engine_mask=first(r))
+            sent += len(_bits(first(r)))
+        tk_id.append(("idr", sum(len(_bits(first(i))) for i in sibs)))
+
     ready = {r: [tk_k, tk_v]}
     if later:
         need("g", [tk_sk, tk_sv])
@@ -125,16 +157,18 @@ def rank_program(g, core, T, topo):
                                               remote_sem=T.sem["ld%d" % r], srcs=[T.kvd[:, :]],
                                               dsts=[T.landd[r] for d in dcs], alu_op=0)], local_sem=T.sem.sent)
         sent += len(_bits(m))
+    tk_mk = emit("g", [t_zero], lambda: g.affine_select(T.maskb[:, :], T.maskb[:, :], [[-1, 128]],
+                                                        AluOpType.is_ge, -30000.0, 0, 1))
     for i in sibs:
         if i > r:
             need("g", [tk_k, tk_v])
             a = topo.addr(cores[i])
-            m = topo.mask(core, cores[i])
+            m = quiet(r)
             g.remote_dma(out_ap=slot(r), in_ap=slot(r), remote_sem=T.sem["fw%d" % r], local_sem=T.sem.sent,
                          pid=a[1], routing_id=a[0], dma_engine_mask=m)
             sent += len(_bits(m))
         else:
-            ready[i] = [("fw%d" % i, len(_bits(topo.mask(cores[i], core))))]
+            ready[i] = [("fw%d" % i, len(_bits(quiet(i))))]
     for ch in reversed(earlier):
         mine = [j for j in members[ch] if lander(j, my_chip) == r]
         lds = {j: ("ld%d" % j, len(_bits(topo.mask(cores[j], core)))) for j in mine}
@@ -192,14 +226,8 @@ def rank_program(g, core, T, topo):
         tok = None
         for b, j in enumerate(steps[t]):
             out = S[:, b * 128:(b + 1) * 128]
-            if j == r:
-                tok = emit("pe", [tk_id, tk_mk],
-                           lambda: g.tensor.matmul(out, T.ident[:, :], T.maskb[:, :], start=True, stop=False), 1, tok)
-                tok = emit("pe", [tk_q] + ready[j],
-                           lambda: g.tensor.matmul(out, T.qs[:, :], kslot(j), start=False, stop=True), 1, tok)
-            else:
-                tok = emit("pe", [tk_q] + ready[j],
-                           lambda: g.tensor.matmul(out, T.qs[:, :], kslot(j), start=True, stop=True), 1, tok)
+            tok = emit("pe", [tk_q] + ready[j],
+                       lambda: g.tensor.matmul(out, T.qs[:, :], kslot(j), start=True, stop=True), 1, tok)
         X[t]["S"] = tok
 
     def maxexp(t):
@@ -207,6 +235,9 @@ def rank_program(g, core, T, topo):
         nb = len(steps[t])
         x = X[t]
         c_m = cols()
+        if t == 0:
+            x["S"] = emit("dve", [x["S"], tk_mk],
+                          lambda: g.vector.tensor_tensor(S[:, 0:128], S[:, 0:128], T.maskb[:, :], op=AluOpType.add))
         tm = emit("dve", [x["S"]], lambda: g.vector.tensor_reduce(st(c_m), S[:, 0:nb * 128], axis=AxisListType.X,
                                                                   op=AluOpType.max, negate=True))
         if t == 0:
@@ -237,7 +268,7 @@ def rank_program(g, core, T, topo):
 
     def rescale_prep(t):
         x, pv = X[t], X[t - 1]
-        x["dg"] = emit("dve", [x["w"], tk_id],
+        x["dg"] = emit("dve", [x["w"]] + tk_id,
                        lambda: g.vector.tensor_scalar(blk(T.dg, t), T.ident[:, :], st(x["cw"]), None,
                                                       op0=AluOpType.mult))
         x["lw"] = emit("dve", [x["w"], pv["L"]],
@@ -249,7 +280,7 @@ def rank_program(g, core, T, topo):
         x["C"] = []
         tts = []
         for b in range(len(steps[t])):
-            tts.append(emit("pe", [x["E"][b], tk_id],
+            tts.append(emit("pe", [x["E"][b]] + tk_id,
                             lambda b=b: g.tensor.transpose(ps_t[b % 2][:, 0:128], blk(T.p, base[t] + b),
                                                            T.ident[:, :])))
         for b in range(len(steps[t])):
@@ -285,13 +316,7 @@ def rank_program(g, core, T, topo):
 
     scores(0)
     maxexp(0)
-    transposes(0)
-    outputs(0)
-    if ns > 1:
-        scores(1)
-        maxexp(1)
-        rescale_prep(1)
-    for t in range(1, ns):
+    for t in range(ns):
         if t + 1 < ns:
             scores(t + 1)
             maxexp(t + 1)

@@ -17,14 +17,21 @@ SCRATCH = {
     "ys": ("sbuf", [128, 128], "bfloat16"),
     "kvd": ("dram", [128, 256], "bfloat16"),
     "landd": ("dram", [N, 128, 256], "bfloat16"),
-    "ps_s0": ("psum", [128, 512], "float32"),
-    "ps_s1": ("psum", [128, 512], "float32"),
+    "kd": ("dram", [128, 128], "bfloat16"),
+    "vd": ("dram", [128, 128], "bfloat16"),
+    "landk": ("dram", [N, 128, 128], "bfloat16"),
+    "landv": ("dram", [N, 128, 128], "bfloat16"),
+    "ps_s00": ("psum", [128, 512], "float32"),
+    "ps_s01": ("psum", [128, 512], "float32"),
+    "ps_s10": ("psum", [128, 512], "float32"),
+    "ps_s11": ("psum", [128, 512], "float32"),
     "ps_t0": ("psum", [128, 1024], "bfloat16"),
     "ps_t1": ("psum", [128, 1024], "bfloat16"),
     "ps_o0": ("psum", [128, 512], "float32"),
     "ps_o1": ("psum", [128, 512], "float32"),
 }
 SEMAPHORES = (["sent", "idr"] + ["ld%d" % j for j in range(N)] + ["fw%d" % j for j in range(N)]
+              + ["%s%d" % (p, j) for p in ("lk", "lv", "fk", "fv") for j in range(N)]
               + ["x%d" % i for i in range(NPOOL)])
 
 
@@ -59,6 +66,9 @@ def rank_program(g, core, T, topo):
     def lander(j, ch):
         m = members[ch]
         return m[members[chip_of[j]].index(j) % len(m)]
+
+    def halved(src, dst):
+        return len(chips) > 2 and src == chips[0] and dst == chips[-1]
 
     def quiet(i):
         ch = chip_of[i]
@@ -119,10 +129,14 @@ def rank_program(g, core, T, topo):
     def vslot(j):
         return T.kv[:, j * 256 + 128:(j + 1) * 256]
 
-    tk_sk = tk_sv = None
+    tk_sk = tk_sv = tk_kd = tk_vd = None
     if later:
         tk_sk = emit("sp", [], lambda: g.sync.dma_start(T.kvd[:, 0:128], T.k[:, :]), 16)
         tk_sv = emit("act", [], lambda: g.scalar.dma_start(T.kvd[:, 128:256], T.v[:, :]), 16)
+    halves = [ch for ch in later if halved(my_chip, ch)]
+    if halves:
+        tk_kd = emit("sp", [], lambda: g.sync.dma_start(T.kd[:, :], T.k[:, :]), 16)
+        tk_vd = emit("act", [], lambda: g.scalar.dma_start(T.vd[:, :], T.v[:, :]), 16)
     tk_k = emit("sp", [], lambda: g.sync.dma_start(kslot(r), T.k[:, :]), 16)
     tk_v = emit("act", [], lambda: g.scalar.dma_start(vslot(r), T.v[:, :]), 16)
     tk_q = emit("sp", [], lambda: g.sync.dma_start(T.qs[:, :], T.q[:, :]), 16)
@@ -146,10 +160,12 @@ def rank_program(g, core, T, topo):
             sent += len(_bits(first(r)))
         tk_id.append(("idr", sum(len(_bits(first(i))) for i in sibs)))
 
-    ready = {r: [tk_k, tk_v]}
+    ready = {}
+    rk = {r: [tk_k]}
+    rv = {r: [tk_v]}
     if later:
         need("g", [tk_sk, tk_sv])
-        dcs = [cores[lander(r, ch)] for ch in later]
+        dcs = [cores[lander(r, ch)] for ch in later if ch not in halves]
         m = topo.mask(core, dcs[0])
         for d in dcs:
             m &= topo.mask(core, d)
@@ -157,6 +173,14 @@ def rank_program(g, core, T, topo):
                                               remote_sem=T.sem["ld%d" % r], srcs=[T.kvd[:, :]],
                                               dsts=[T.landd[r] for d in dcs], alu_op=0)], local_sem=T.sem.sent)
         sent += len(_bits(m))
+        for ch in halves:
+            d = cores[lander(r, ch)]
+            a = topo.addr(d)
+            for tk, src, dst, nm in ((tk_kd, T.kd, T.landk, "lk"), (tk_vd, T.vd, T.landv, "lv")):
+                need("g", [tk])
+                g.remote_dma(out_ap=dst[r], in_ap=src[:, :], remote_sem=T.sem["%s%d" % (nm, r)],
+                             local_sem=T.sem.sent, pid=a[1], routing_id=a[0], dma_engine_mask=topo.mask(core, d))
+                sent += len(_bits(topo.mask(core, d)))
     tk_mk = emit("g", [t_zero], lambda: g.affine_select(T.maskb[:, :], T.maskb[:, :], [[-1, 128]],
                                                         AluOpType.is_ge, -30000.0, 0, 1))
     for i in sibs:
@@ -171,6 +195,22 @@ def rank_program(g, core, T, topo):
             ready[i] = [("fw%d" % i, len(_bits(quiet(i))))]
     for ch in reversed(earlier):
         mine = [j for j in members[ch] if lander(j, my_chip) == r]
+        if halved(ch, my_chip):
+            for nm, part, land, rd in (("k", kslot, T.landk, rk), ("v", vslot, T.landv, rv)):
+                for j in mine:
+                    tl = ("l%s%d" % (nm, j), len(_bits(topo.mask(cores[j], core))))
+                    rd[j] = [emit("sp", [tl], lambda: g.sync.dma_start(part(j), land[j]), 16)]
+                    need("g", [tl])
+                    for i in sibs:
+                        a = topo.addr(cores[i])
+                        m = topo.mask(core, cores[i])
+                        g.remote_dma(out_ap=part(j), in_ap=land[j], remote_sem=T.sem["f%s%d" % (nm, j)],
+                                     local_sem=T.sem.sent, pid=a[1], routing_id=a[0], dma_engine_mask=m)
+                        sent += len(_bits(m))
+                for j in members[ch]:
+                    if j not in mine:
+                        rd[j] = [("f%s%d" % (nm, j), len(_bits(topo.mask(cores[lander(j, my_chip)], core))))]
+            continue
         lds = {j: ("ld%d" % j, len(_bits(topo.mask(cores[j], core)))) for j in mine}
         for j in mine:
             ready[j] = [emit("sp", [lds[j]], lambda j=j: g.sync.dma_start(slot(j), T.landd[j]), 16)]
@@ -194,10 +234,14 @@ def rank_program(g, core, T, topo):
                 ready[j] = [("fw%d" % j, len(_bits(topo.mask(cores[lr], core))) // parts)]
     if sent:
         need("g", [("sent", sent)])
+    for j in ready:
+        rk[j] = ready[j]
+        rv[j] = ready[j]
 
-    steps = [[r] + [i for i in sibs if i < r]] + [list(reversed(members[ch])) for ch in reversed(earlier)]
+    steps = [[r] + [i for i in sibs if i < r]] + [sorted(members[ch], key=lambda j: (lander(j, my_chip) != r, -j))
+                                                  for ch in reversed(earlier)]
     ns = len(steps)
-    ps_s = [T.ps_s0, T.ps_s1]
+    ps_s = [[T.ps_s00, T.ps_s01], [T.ps_s10, T.ps_s11]]
     ps_t = [T.ps_t0, T.ps_t1]
     ps_o = [T.ps_o0, T.ps_o1]
     col = [0]
@@ -205,6 +249,13 @@ def rank_program(g, core, T, topo):
     def cols(k=1):
         c = col[0]
         col[0] += k
+        return c
+
+    mcol = [64]
+
+    def mcols(k=1):
+        c = mcol[0]
+        mcol[0] += k
         return c
 
     def st(c, k=1):
@@ -222,47 +273,49 @@ def rank_program(g, core, T, topo):
     X = [{} for _ in steps]
 
     def scores(t):
-        S = ps_s[t % 2]
-        tok = None
+        x = X[t]
+        x["S"] = {}
         for b, j in enumerate(steps[t]):
-            out = S[:, b * 128:(b + 1) * 128]
-            tok = emit("pe", [tk_q] + ready[j],
-                       lambda: g.tensor.matmul(out, T.qs[:, :], kslot(j), start=True, stop=True), 1, tok)
-        X[t]["S"] = tok
+            x["S"][b] = emit("pe", [tk_q] + rk[j],
+                             lambda: g.tensor.matmul(ps_s[t % 2][b][:, 0:128], T.qs[:, :], kslot(j),
+                                                     start=True, stop=True))
 
     def maxexp(t):
-        S = ps_s[t % 2]
         nb = len(steps[t])
         x = X[t]
-        c_m = cols()
-        if t == 0:
-            x["S"] = emit("dve", [x["S"], tk_mk],
-                          lambda: g.vector.tensor_tensor(S[:, 0:128], S[:, 0:128], T.maskb[:, :], op=AluOpType.add))
-        tm = emit("dve", [x["S"]], lambda: g.vector.tensor_reduce(st(c_m), S[:, 0:nb * 128], axis=AxisListType.X,
-                                                                  op=AluOpType.max, negate=True))
-        if t == 0:
-            x["cM"], x["M"] = c_m, tm
-            x["cl"] = cols(nb)
-            x["nl"] = nb
-            l0 = x["cl"]
+        c_m = mcols(nb)
+        tms = []
+        for b in range(nb):
+            Sb = ps_s[t % 2][b][:, 0:128]
+            if t == 0 and b == 0:
+                x["S"][0] = emit("dve", [x["S"][0], tk_mk],
+                                 lambda: g.vector.tensor_tensor(Sb, Sb, T.maskb[:, :], op=AluOpType.add))
+            tms.append(emit("dve", [x["S"][b]],
+                            lambda: g.vector.tensor_reduce(st(c_m + b), Sb, axis=AxisListType.X,
+                                                           op=AluOpType.max, negate=True)))
+        if t == 0 and nb == 1:
+            x["cM"], x["M"] = c_m, tms[0]
         else:
-            pv = X[t - 1]
-            c_M = cols()
+            lo = c_m if t == 0 else X[t - 1]["cM"]
+            c_M = mcols()
             x["cM"] = c_M
-            x["M"] = emit("dve", [tm, pv["M"]], lambda: g.vector.tensor_tensor(st(c_M), st(c_m), st(pv["cM"]),
-                                                                              op=AluOpType.min))
+            x["M"] = emit("dve", tms + ([] if t == 0 else [X[t - 1]["M"]]),
+                          lambda: g.vector.tensor_reduce(st(c_M), st(lo, c_M - lo), axis=AxisListType.X,
+                                                         op=AluOpType.min))
+        if t > 0:
+            pv = X[t - 1]
             c_w = cols()
             x["cw"] = c_w
             x["w"] = emit("act", [x["M"], pv["M"]],
                           lambda: g.scalar.activation(st(c_w), st(pv["cM"]), ActivationFunctionType.Exp,
-                                                      bias=st(c_M), scale=-1.0))
-            x["cl"] = cols(nb + 1)
-            x["nl"] = nb + 1
-            l0 = x["cl"] + 1
+                                                      bias=st(x["cM"]), scale=-1.0))
+        x["nl"] = nb if t == 0 else nb + 1
+        x["cl"] = cols(x["nl"])
+        l0 = x["cl"] + x["nl"] - nb
         x["E"] = []
         for b in range(nb):
-            x["E"].append(emit("act", [x["M"], x["S"]],
-                               lambda b=b: g.scalar.activation(blk(T.p, base[t] + b), S[:, b * 128:(b + 1) * 128],
+            x["E"].append(emit("act", [x["M"], x["S"][b]],
+                               lambda b=b: g.scalar.activation(blk(T.p, base[t] + b), ps_s[t % 2][b][:, 0:128],
                                                                ActivationFunctionType.Exp, bias=st(x["cM"]),
                                                                scale=1.0, accum_out=st(l0 + b))))
 
@@ -284,8 +337,13 @@ def rank_program(g, core, T, topo):
                             lambda b=b: g.tensor.transpose(ps_t[b % 2][:, 0:128], blk(T.p, base[t] + b),
                                                            T.ident[:, :])))
         for b in range(len(steps[t])):
-            x["C"].append(emit("dve", [tts[b]],
-                               lambda b=b: g.vector.tensor_copy(blk(T.pt, base[t] + b), ps_t[b % 2][:, 0:128])))
+            if t == ns - 1 and b == len(steps[t]) - 1:
+                x["C"].append(emit("act", [tts[b]],
+                                   lambda b=b: g.scalar.activation(blk(T.pt, base[t] + b), ps_t[b % 2][:, 0:128],
+                                                                   ActivationFunctionType.Copy)))
+            else:
+                x["C"].append(emit("dve", [tts[b]],
+                                   lambda b=b: g.vector.tensor_copy(blk(T.pt, base[t] + b), ps_t[b % 2][:, 0:128])))
         c_L = cols()
         x["cL"] = c_L
         x["L"] = emit("dve", x["E"] + [x.get("lw")],
@@ -301,7 +359,7 @@ def rank_program(g, core, T, topo):
             tok = emit("pe", [x["dg"], X[t - 1]["O"]],
                        lambda: g.tensor.matmul(O, blk(T.dg, t), blk(T.op, t - 1), start=True, stop=False), 1, tok)
         for b, j in enumerate(steps[t]):
-            tok = emit("pe", [x["C"][b]] + ready[j],
+            tok = emit("pe", [x["C"][b]] + rv[j],
                        lambda b=b, j=j: g.tensor.matmul(O, blk(T.pt, base[t] + b), vslot(j),
                                                         start=(t == 0 and b == 0), stop=(b == nb - 1)), 1, tok)
         if t + 1 < ns:
@@ -314,13 +372,14 @@ def rank_program(g, core, T, topo):
             td = emit("sp", [ty], lambda: g.sync.dma_start(T.y[:, :], T.ys[:, :]), 16)
             need("sp", [td])
 
-    scores(0)
-    maxexp(0)
+    for t in range(min(2, ns)):
+        scores(t)
+        maxexp(t)
     for t in range(ns):
-        if t + 1 < ns:
-            scores(t + 1)
-            maxexp(t + 1)
         transposes(t)
         if t + 1 < ns:
             rescale_prep(t + 1)
+        if t + 2 < ns:
+            scores(t + 2)
+            maxexp(t + 2)
         outputs(t)

from concourse.bass import DstId, RemoteDMATransfer
from concourse.mybir import AluOpType, AxisListType, ActivationFunctionType

N = 8
NPOOL = 96

SCRATCH = {
    "qs": ("sbuf", [128, 128], "bfloat16"),
    "kv": ("sbuf", [128, N * 256], "bfloat16"),
    "ident": ("sbuf", [128, 128], "bfloat16"),
    "maskb": ("sbuf", [128, 128], "bfloat16"),
    "p": ("sbuf", [128, N * 128], "bfloat16"),
    "pt": ("sbuf", [128, N * 128], "bfloat16"),
    "dg": ("sbuf", [128, N * 128], "bfloat16"),
    "op": ("sbuf", [128, N * 128], "bfloat16"),
    "st": ("sbuf", [128, 96], "float32"),
    "ys": ("sbuf", [128, 128], "bfloat16"),
    "kvd": ("dram", [128, 256], "bfloat16"),
    "landd": ("dram", [N, 128, 256], "bfloat16"),
    "kd": ("dram", [128, 128], "bfloat16"),
    "vd": ("dram", [128, 128], "bfloat16"),
    "landk": ("dram", [N, 128, 128], "bfloat16"),
    "landv": ("dram", [N, 128, 128], "bfloat16"),
    "ps_s00": ("psum", [128, 512], "float32"),
    "ps_s01": ("psum", [128, 512], "float32"),
    "ps_s10": ("psum", [128, 512], "float32"),
    "ps_s11": ("psum", [128, 512], "float32"),
    "ps_t0": ("psum", [128, 1024], "bfloat16"),
    "ps_t1": ("psum", [128, 1024], "bfloat16"),
    "ps_o0": ("psum", [128, 512], "float32"),
    "ps_o1": ("psum", [128, 512], "float32"),
}
SEMAPHORES = (["sent", "idr"] + ["ld%d" % j for j in range(N)] + ["fw%d" % j for j in range(N)]
              + ["%s%d" % (p, j) for p in ("lk", "lv", "fk", "fv") for j in range(N)]
              + ["x%d" % i for i in range(NPOOL)])


def _bits(mask):
    return [b for b in range(mask.bit_length()) if (mask >> b) & 1]


def _part(mask, k, parts):
    bs = _bits(mask)
    w = len(bs) // parts
    return sum(1 << b for b in bs[k * w:(k + 1) * w])


def rank_program(g, core, T, topo):
    r = T.rank_of(core)
    if r is None:
        return
    cores = list(T.cores)
    n = len(cores)
    chip_of = [topo.chip(c) for c in cores]
    chips = []
    for ch in chip_of:
        if ch not in chips:
            chips.append(ch)
    members = {ch: [i for i in range(n) if chip_of[i] == ch] for ch in chips}
    my_chip = chip_of[r]
    my_pos = chips.index(my_chip)
    later = chips[my_pos + 1:]
    earlier = chips[:my_pos]
    sibs = [i for i in members[my_chip] if i != r]

    def lander(j, ch):
        m = members[ch]
        return m[members[chip_of[j]].index(j) % len(m)]

    def halved(src, dst):
        return len(chips) > 2 and src == chips[0] and dst == chips[-1]

    def quiet(i):
        ch = chip_of[i]
        on = 0
        for x in members[ch]:
            if x != i:
                mk = topo.mask(cores[i], cores[x])
                on = mk if not on else on & mk
        off = 0
        for c2 in chips[chips.index(ch) + 1:]:
            off |= topo.mask(cores[i], cores[lander(i, c2)])
        rest = on & ~off
        return rest if len(_bits(rest)) in (1, 2, 4, 8, 16) else on

    def first(i):
        ch = chip_of[i]
        m = 0
        for x in members[ch]:
            if x != i:
                mk = topo.mask(cores[i], cores[x])
                m = mk if not m else m & mk
        for c2 in chips[chips.index(ch) + 1:]:
            m &= topo.mask(cores[i], cores[lander(i, c2)])
        return m

    def dst_id(c):
        a = topo.addr(c)
        return DstId(rid=a[0], pnc=a[1])

    eng = {"pe": g.tensor, "dve": g.vector, "act": g.scalar, "sp": g.sync, "g": g}
    seen = {k: {} for k in eng}
    cnt = [0]

    def need(q, toks):
        for t in toks:
            if t is None:
                continue
            nm, v = t
            if seen[q].get(nm, 0) < v:
                eng[q].wait_ge(T.sem[nm], v)
                seen[q][nm] = v

    def emit(q, toks, fn, inc=1, tok=None):
        need(q, toks)
        ins = fn()
        if tok is None:
            tok = ("x%d" % cnt[0], 0)
            cnt[0] += 1
        ins.then_inc(T.sem[tok[0]], inc)
        return (tok[0], tok[1] + inc)

    def slot(j):
        return T.kv[:, j * 256:(j + 1) * 256]

    def kslot(j):
        return T.kv[:, j * 256:j * 256 + 128]

    def vslot(j):
        return T.kv[:, j * 256 + 128:(j + 1) * 256]

    tk_sk = tk_sv = tk_kd = tk_vd = None
    if later:
        tk_sk = emit("sp", [], lambda: g.sync.dma_start(T.kvd[:, 0:128], T.k[:, :]), 16)
        tk_sv = emit("act", [], lambda: g.scalar.dma_start(T.kvd[:, 128:256], T.v[:, :]), 16)
    halves = [ch for ch in later if halved(my_chip, ch)]
    if halves:
        tk_kd = emit("sp", [], lambda: g.sync.dma_start(T.kd[:, :], T.k[:, :]), 16)
        tk_vd = emit("act", [], lambda: g.scalar.dma_start(T.vd[:, :], T.v[:, :]), 16)
    tk_k = emit("sp", [], lambda: g.sync.dma_start(kslot(r), T.k[:, :]), 16)
    tk_v = emit("act", [], lambda: g.scalar.dma_start(vslot(r), T.v[:, :]), 16)
    tk_q = emit("sp", [], lambda: g.sync.dma_start(T.qs[:, :], T.q[:, :]), 16)

    grp = members[my_chip]
    w_id = 128 // len(grp)
    c0 = grp.index(r) * w_id
    own_id = T.ident[:, c0:c0 + w_id]
    sent = 0
    t_one = emit("dve", [], lambda: g.vector.memset(own_id, 1.0))
    t_zero = emit("dve", [], lambda: g.vector.memset(T.maskb[:, :], 0.0))
    t_own = emit("g", [t_one], lambda: g.affine_select(own_id, own_id, [[-1, w_id]],
                                                       AluOpType.is_equal, 0.0, -c0, 1))
    tk_id = [t_own]
    if sibs:
        need("g", [t_own])
        for i in sibs:
            a = topo.addr(cores[i])
            g.remote_dma(out_ap=own_id, in_ap=own_id, remote_sem=T.sem.idr, local_sem=T.sem.sent,
                         pid=a[1], routing_id=a[0], dma_engine_mask=first(r))
            sent += len(_bits(first(r)))
        tk_id.append(("idr", sum(len(_bits(first(i))) for i in sibs)))

    ready = {}
    rk = {r: [tk_k]}
    rv = {r: [tk_v]}
    if later:
        need("g", [tk_sk, tk_sv])
        dcs = [cores[lander(r, ch)] for ch in later if ch not in halves]
        m = topo.mask(core, dcs[0])
        for d in dcs:
            m &= topo.mask(core, d)
        g.remote_dma_fused([RemoteDMATransfer(dst_ids=[dst_id(d) for d in dcs], dma_engine_mask=m,
                                              remote_sem=T.sem["ld%d" % r], srcs=[T.kvd[:, :]],
                                              dsts=[T.landd[r] for d in dcs], alu_op=0)], local_sem=T.sem.sent)
        sent += len(_bits(m))
        for ch in halves:
            d = cores[lander(r, ch)]
            a = topo.addr(d)
            for tk, src, dst, nm in ((tk_kd, T.kd, T.landk, "lk"), (tk_vd, T.vd, T.landv, "lv")):
                need("g", [tk])
                g.remote_dma(out_ap=dst[r], in_ap=src[:, :], remote_sem=T.sem["%s%d" % (nm, r)],
                             local_sem=T.sem.sent, pid=a[1], routing_id=a[0], dma_engine_mask=topo.mask(core, d))
                sent += len(_bits(topo.mask(core, d)))
    tk_mk = emit("g", [t_zero], lambda: g.affine_select(T.maskb[:, :], T.maskb[:, :], [[-1, 128]],
                                                        AluOpType.is_ge, -30000.0, 0, 1))
    for i in sibs:
        if i > r:
            need("g", [tk_k, tk_v])
            a = topo.addr(cores[i])
            m = quiet(r)
            g.remote_dma(out_ap=slot(r), in_ap=slot(r), remote_sem=T.sem["fw%d" % r], local_sem=T.sem.sent,
                         pid=a[1], routing_id=a[0], dma_engine_mask=m)
            sent += len(_bits(m))
        else:
            ready[i] = [("fw%d" % i, len(_bits(quiet(i))))]
    for ch in reversed(earlier):
        mine = [j for j in members[ch] if lander(j, my_chip) == r]
        if halved(ch, my_chip):
            for nm, part, land, rd in (("k", kslot, T.landk, rk), ("v", vslot, T.landv, rv)):
                for j in mine:
                    tl = ("l%s%d" % (nm, j), len(_bits(topo.mask(cores[j], core))))
                    rd[j] = [emit("sp", [tl], lambda: g.sync.dma_start(part(j), land[j]), 16)]
                    need("g", [tl])
                    for i in sibs:
                        a = topo.addr(cores[i])
                        m = topo.mask(core, cores[i])
                        g.remote_dma(out_ap=part(j), in_ap=land[j], remote_sem=T.sem["f%s%d" % (nm, j)],
                                     local_sem=T.sem.sent, pid=a[1], routing_id=a[0], dma_engine_mask=m)
                        sent += len(_bits(m))
                for j in members[ch]:
                    if j not in mine:
                        rd[j] = [("f%s%d" % (nm, j), len(_bits(topo.mask(cores[lander(j, my_chip)], core))))]
            continue
        lds = {j: ("ld%d" % j, len(_bits(topo.mask(cores[j], core)))) for j in mine}
        for j in mine:
            ready[j] = [emit("sp", [lds[j]], lambda j=j: g.sync.dma_start(slot(j), T.landd[j]), 16)]
        if mine and sibs:
            need("g", [lds[j] for j in mine])
            m = topo.mask(core, cores[sibs[0]])
            for i in sibs:
                m &= topo.mask(core, cores[i])
            trs = []
            for x, j in enumerate(mine):
                mm = _part(m, x, len(mine))
                trs.append(RemoteDMATransfer(dst_ids=[dst_id(cores[i]) for i in sibs], dma_engine_mask=mm,
                                             remote_sem=T.sem["fw%d" % j], srcs=[T.landd[j]],
                                             dsts=[slot(j) for i in sibs], alu_op=0))
                sent += len(_bits(mm))
            g.remote_dma_fused(trs, local_sem=T.sem.sent)
        for j in members[ch]:
            if j not in mine:
                lr = lander(j, my_chip)
                parts = len([x for x in members[ch] if lander(x, my_chip) == lr])
                ready[j] = [("fw%d" % j, len(_bits(topo.mask(cores[lr], core))) // parts)]
    if sent:
        need("g", [("sent", sent)])
    for j in ready:
        rk[j] = ready[j]
        rv[j] = ready[j]

    steps = [[r] + [i for i in sibs if i < r]] + [sorted(members[ch], key=lambda j: (lander(j, my_chip) != r, -j))
                                                  for ch in reversed(earlier)]
    ns = len(steps)
    ps_s = [[T.ps_s00, T.ps_s01], [T.ps_s10, T.ps_s11]]
    ps_t = [T.ps_t0, T.ps_t1]
    ps_o = [T.ps_o0, T.ps_o1]
    col = [0]

    def cols(k=1):
        c = col[0]
        col[0] += k
        return c

    mcol = [64]

    def mcols(k=1):
        c = mcol[0]
        mcol[0] += k
        return c

    def st(c, k=1):
        return T.st[:, c:c + k]

    base = []
    b0 = 0
    for s in steps:
        base.append(b0)
        b0 += len(s)

    def blk(buf, i):
        return buf[:, i * 128:(i + 1) * 128]

    X = [{} for _ in steps]

    def scores(t):
        x = X[t]
        x["S"] = {}
        for b, j in enumerate(steps[t]):
            x["S"][b] = emit("pe", [tk_q] + rk[j],
                             lambda: g.tensor.matmul(ps_s[t % 2][b][:, 0:128], T.qs[:, :], kslot(j),
                                                     start=True, stop=True))

    def maxexp(t):
        nb = len(steps[t])
        x = X[t]
        c_m = mcols(nb)
        tms = []
        for b in range(nb):
            Sb = ps_s[t % 2][b][:, 0:128]
            if t == 0 and b == 0:
                x["S"][0] = emit("dve", [x["S"][0], tk_mk],
                                 lambda: g.vector.tensor_tensor(Sb, Sb, T.maskb[:, :], op=AluOpType.add))
            tms.append(emit("dve", [x["S"][b]],
                            lambda: g.vector.tensor_reduce(st(c_m + b), Sb, axis=AxisListType.X,
                                                           op=AluOpType.max, negate=True)))
        if t == 0 and nb == 1:
            x["cM"], x["M"] = c_m, tms[0]
        else:
            lo = c_m if t == 0 else X[t - 1]["cM"]
            c_M = mcols()
            x["cM"] = c_M
            x["M"] = emit("dve", tms + ([] if t == 0 else [X[t - 1]["M"]]),
                          lambda: g.vector.tensor_reduce(st(c_M), st(lo, c_M - lo), axis=AxisListType.X,
                                                         op=AluOpType.min))
        if t > 0:
            pv = X[t - 1]
            c_w = cols()
            x["cw"] = c_w
            x["w"] = emit("act", [x["M"], pv["M"]],
                          lambda: g.scalar.activation(st(c_w), st(pv["cM"]), ActivationFunctionType.Exp,
                                                      bias=st(x["cM"]), scale=-1.0))
        x["nl"] = nb if t == 0 else nb + 1
        x["cl"] = cols(x["nl"])
        l0 = x["cl"] + x["nl"] - nb
        x["E"] = []
        for b in range(nb):
            x["E"].append(emit("act", [x["M"], x["S"][b]],
                               lambda b=b: g.scalar.activation(blk(T.p, base[t] + b), ps_s[t % 2][b][:, 0:128],
                                                               ActivationFunctionType.Exp, bias=st(x["cM"]),
                                                               scale=1.0, accum_out=st(l0 + b))))

    def rescale_prep(t):
        x, pv = X[t], X[t - 1]
        x["dg"] = emit("dve", [x["w"]] + tk_id,
                       lambda: g.vector.tensor_scalar(blk(T.dg, t), T.ident[:, :], st(x["cw"]), None,
                                                      op0=AluOpType.mult))
        x["lw"] = emit("dve", [x["w"], pv["L"]],
                       lambda: g.vector.tensor_scalar(st(x["cl"]), st(pv["cL"]), st(x["cw"]), None,
                                                      op0=AluOpType.mult))

    def transposes(t):
        x = X[t]
        x["C"] = []
        tts = []
        for b in range(len(steps[t])):
            tts.append(emit("pe", [x["E"][b]] + tk_id,
                            lambda b=b: g.tensor.transpose(ps_t[b % 2][:, 0:128], blk(T.p, base[t] + b),
                                                           T.ident[:, :])))
        for b in range(len(steps[t])):
            if t == ns - 1 and b == len(steps[t]) - 1:
                x["C"].append(emit("act", [tts[b]],
                                   lambda b=b: g.scalar.activation(blk(T.pt, base[t] + b), ps_t[b % 2][:, 0:128],
                                                                   ActivationFunctionType.Copy)))
            else:
                x["C"].append(emit("dve", [tts[b]],
                                   lambda b=b: g.vector.tensor_copy(blk(T.pt, base[t] + b), ps_t[b % 2][:, 0:128])))
        c_L = cols()
        x["cL"] = c_L
        x["L"] = emit("dve", x["E"] + [x.get("lw")],
                      lambda: g.vector.tensor_reduce(st(c_L), st(x["cl"], x["nl"]), axis=AxisListType.X,
                                                     op=AluOpType.add))

    def outputs(t):
        x = X[t]
        O = ps_o[t % 2][:, 0:128]
        nb = len(steps[t])
        tok = None
        if t > 0:
            tok = emit("pe", [x["dg"], X[t - 1]["O"]],
                       lambda: g.tensor.matmul(O, blk(T.dg, t), blk(T.op, t - 1), start=True, stop=False), 1, tok)
        for b, j in enumerate(steps[t]):
            tok = emit("pe", [x["C"][b]] + rv[j],
                       lambda b=b, j=j: g.tensor.matmul(O, blk(T.pt, base[t] + b), vslot(j),
                                                        start=(t == 0 and b == 0), stop=(b == nb - 1)), 1, tok)
        if t + 1 < ns:
            x["O"] = emit("dve", [tok], lambda: g.vector.tensor_copy(blk(T.op, t), O))
        else:
            c_r = cols()
            tr = emit("dve", [x["L"]], lambda: g.vector.reciprocal(st(c_r), st(x["cL"])))
            ty = emit("dve", [tr, tok], lambda: g.vector.tensor_scalar(T.ys[:, :], O, st(c_r), None,
                                                                       op0=AluOpType.mult))
            td = emit("sp", [ty], lambda: g.sync.dma_start(T.y[:, :], T.ys[:, :]), 16)
            need("sp", [td])

    for t in range(min(2, ns)):
        scores(t)
        maxexp(t)
    for t in range(ns):
        transposes(t)
        if t + 1 < ns:
            rescale_prep(t + 1)
        if t + 2 < ns:
            scores(t + 2)
            maxexp(t + 2)
        outputs(t)
